import numpy as np
import ml_dtypes


def mxq(x, axis, fmt="e4m3"):
    dtype, down = {"e4m3": (ml_dtypes.float8_e4m3fn, 7), "e5m2": (ml_dtypes.float8_e5m2, 14)}[fmt]
    v = np.moveaxis(np.asarray(x, np.float32).astype(ml_dtypes.bfloat16).astype(np.float64), axis, -1)
    blocks = v.reshape(v.shape[:-1] + (-1, 32))
    amax = np.abs(blocks).max(-1, keepdims=True)
    byte = np.maximum(np.where(amax > 0, np.frexp(amax)[1] - 1 + 127, 0) - down, 1)
    scale = np.exp2(byte - 127.0)
    codes = (blocks / scale).astype(np.float32).astype(dtype).astype(np.float64)
    return np.moveaxis((codes * scale).reshape(v.shape), -1, axis)


WIDE = False


def mx_kscale(k):
    if not WIDE:
        return np.ones(k)
    levels = np.array([10, -10, 5, -5, 0])
    if k % 512:
        return np.exp2(np.random.permutation(np.resize(levels, k // 32))).repeat(32)
    a = np.empty((k // 512, 16))
    for p in range(k // 512):
        a[p, :8] = np.random.permutation(np.resize(levels, 8))
        for g in range(8):
            far = levels[np.abs(levels - a[p, g]) >= 10]
            a[p, g + 8] = far[np.random.randint(len(far))]
    return np.exp2(a.ravel()).repeat(32)


def f64(x):
    return np.asarray(x).astype(np.float64)


def striped(idx):
    return np.tile(np.asarray(idx).reshape(-1, 16).T, (8, 1)).astype(np.uint16)


def unstriped(offs):
    return offs[:16].T.reshape(-1).astype(np.int64)


E2M1 = np.array([0.0, 0.5, 1.0, 1.5, 2.0, 3.0, 4.0, 6.0, -0.0, -0.5, -1.0, -1.5, -2.0, -3.0, -4.0, -6.0])


def pack_weight(w, fmt):
    k, n = w.shape
    w = f64(np.asarray(w, np.float32).astype(ml_dtypes.bfloat16)).reshape(k // 32, 32, n)
    amax = np.abs(w).max(1)
    if fmt == "e4m3":
        byte = np.frexp(amax)[1] - 1 + 127 - 7
    else:
        mant, ex = np.frexp(amax / 6.0)
        byte = np.where(mant > 0.5, ex, ex - 1) + 127
    byte = np.clip(np.where(amax > 0, byte, 1), 1, 254)
    scaled = (w * np.exp2(127.0 - byte)[:, None, :]).reshape(k, n).astype(np.float32)
    by_word = np.ascontiguousarray(scaled.reshape(k // 512, 128, 4, n).transpose(0, 1, 3, 2))
    if fmt == "e4m3":
        words = by_word.astype(ml_dtypes.float8_e4m3fn).view(np.uint8)
    else:
        c = by_word.astype(ml_dtypes.float4_e2m1fn).view(np.uint8) & 0xF
        words = (c[..., 0::2] | (c[..., 1::2] << 4)).reshape(k // 512, 128, 2 * n)
    return np.ascontiguousarray(words), np.ascontiguousarray(byte.astype(np.uint8).reshape(k // 512, 16, n))


def unpack_weight(words, scales, fmt):
    g, _, n = scales.shape
    words = np.ascontiguousarray(words).reshape(g, 128, n, -1)
    if fmt == "e4m3":
        vals = words.view(ml_dtypes.float8_e4m3fn).astype(np.float64)
    else:
        nib = np.empty((g, 128, n, 4), np.uint8)
        nib[..., 0::2] = words & 0xF
        nib[..., 1::2] = words >> 4
        vals = E2M1[nib]
    vals = vals * np.repeat(np.exp2(scales.astype(np.float64) - 127.0), 8, axis=1)[..., None]
    return vals.transpose(0, 1, 3, 2).reshape(g * 512, n)


def bf(x):
    return np.asarray(x, np.float32).astype(ml_dtypes.bfloat16)


def planes(Y):
    r, m = Y.shape
    b = f64(bf(Y)).reshape(r // 32, 32, m)
    amax = np.abs(b).max(1)
    byte = np.clip(np.where(amax > 0, np.frexp(amax)[1] - 1 + 127 - 7, 1), 1, 254)
    codes = (b * np.exp2(127.0 - byte)[:, None, :]).reshape(r, m).astype(np.float32).astype(ml_dtypes.float8_e4m3fn).view(np.uint8)
    words = codes.reshape(r // 512, 128, 4, m).transpose(0, 1, 3, 2)
    return np.ascontiguousarray(words), np.ascontiguousarray(byte.astype(np.uint8).reshape(r // 512, 16, m))


D, T, I, Q, E, U = 512, 2048, 512, 256, 512, 512


def setup_inputs():
    n = np.random.standard_normal
    idx = np.random.permutation(T)[:I]
    idx2 = np.random.randint(0, U, I)
    fd = mx_kscale(D)
    fi = mx_kscale(I)
    ti = np.ones(T)
    ti[idx] = fi
    keysp = pack_weight(n((D, T)) / fd[:, None], "e2m1")
    return {
        "query": (n((D, Q)) * 0.25 / np.sqrt(D) * fd[:, None]).astype(np.float32),
        "keys_words": keysp[0],
        "keys_scales": keysp[1],
        "pquery": (n((D, Q)) * 1.0 / np.sqrt(D) * fd[:, None]).astype(np.float32),
        "pgsum": (n((D, U)) / fd[:, None]).astype(np.float32),
        "th": (np.random.uniform(-0.8, 0.2, (Q, 1))).astype(np.float32),
        "size": (np.random.uniform(0.5, 2.0, (1, I)) * fi).astype(np.float32),
        "vals": (n((E, T)) / ti).astype(np.float32),
        "offs": striped(idx),
        "offs2": striped(idx2),
    }


def reference(query, keys_words, keys_scales, pquery, pgsum, th, size, vals, offs, offs2):
    idx = unstriped(offs)
    idx2 = unstriped(offs2)
    keysu = unpack_weight(keys_words, keys_scales, "e2m1")
    pqueryq = mxq(f64(pquery), 0, "e4m3")
    pgsumq = mxq(f64(pgsum), 0, "e4m3")
    b = pqueryq.T @ pgsumq
    ex = np.maximum(b - f64(th), 0.05)
    queryq = mxq(f64(query), 0, "e4m3")
    keysidxg = keysu[:, idx]
    a = queryq.T @ keysidxg
    p = np.exp(a - np.max(a, axis=1, keepdims=True)) * ex[:, idx2]
    w = p * f64(size) / np.sum(p, axis=1, keepdims=True)
    wt = w.T
    vt = f64(vals)[:, idx].T
    vtq = mxq(vt, 0, "e4m3")
    wtq = mxq(wt, 0, "e4m3")
    o = vtq.T @ wtq
    words, scales = planes(o)
    return o, words, scales

@@ -1,0 +1,203 @@
+from contextlib import ExitStack
+
+import concourse.mybir as mybir
+from concourse.masks import make_identity
+
+D, T, I, Q, E, U = 512, 2048, 512, 256, 512, 512
+FLOPS = 2 * D * Q * U + 2 * D * Q * I + 2 * I * E * Q
+
+F32 = mybir.dt.float32
+BF16 = mybir.dt.bfloat16
+I32 = mybir.dt.int32
+U32 = mybir.dt.uint32
+U16 = mybir.dt.uint16
+U8 = mybir.dt.uint8
+FP8X4 = mybir.dt.float8_e4m3fn_x4
+FP4X4 = mybir.dt.float4_e2m1fn_x4
+ALU = mybir.AluOpType
+ACT = mybir.ActivationFunctionType
+
+P = 128
+PACK = 4
+HALVES = Q // P
+FLOOR = 0.05
+SPARE = 16
+
+
+def tile_attend_pagethreshold_pl_kernel(tc, query, keys_words, keys_scales, pquery, pgsum, th, size, vals,
+                                         offs, offs2, out_0, out_1, out_2):
+    nc = tc.nc
+    with ExitStack() as ctx:
+        sb = ctx.enter_context(tc.tile_pool(name="sb", bufs=1))
+        ps = ctx.enter_context(tc.psum_pool(name="ps", bufs=1))
+
+        def interleave(engine, grouped, raw):
+            dst = grouped.rearrange("p (c i) t -> p c t i", i=4)
+            src = raw.rearrange("p t (c i) -> p c t i", i=4)
+            if engine == "scalar":
+                nc.scalar.activation(dst, src, ACT.Copy)
+            else:
+                nc.vector.tensor_copy(dst, src)
+
+        def quantise(name, grouped, width):
+            codes = sb.tile([P, width], U32, name=name + "_codes", align_bytes=64)
+            scales = sb.tile([P, width], U8, name=name + "_scales", align_bytes=64)
+            nc.vector.quantize_mx(out=codes[:].bitcast(FP8X4), scales=scales[:], in_=grouped)
+            return codes, scales
+
+        key_scale_pool = sb.tile([P, T], U8, name="key_scale_pool")
+        nc.vector.memset(key_scale_pool[:].bitcast(I32), 0)
+        slots = sb.tile([P, I // 16], U16, name="slots")
+        nc.sync.dma_start(slots[:], offs)
+        key_word_pool = sb.tile([P, T], U16, name="key_word_pool")
+        nc.sync.dma_start(key_word_pool[:].bitcast(I32), keys_words[0].bitcast(I32))
+        for g in range(4):
+            nc.sync.dma_start(key_scale_pool[32 * g:32 * g + 4, :].bitcast(I32),
+                              keys_scales[0, 4 * g:4 * g + 4, :].bitcast(I32))
+        query_raw = sb.tile([P, PACK, Q], F32, name="query_raw")
+        nc.sync.dma_start(query_raw[:], query.rearrange("(p t) q -> p t q", t=PACK))
+        pquery_raw = sb.tile([P, PACK, Q], F32, name="pquery_raw")
+        nc.sync.dma_start(pquery_raw[:], pquery.rearrange("(p t) q -> p t q", t=PACK))
+        pg_raw = []
+        for c in range(2):
+            raw = sb.tile([P, PACK, U // 2], F32, name="pg_raw%d" % c)
+            nc.sync.dma_start(raw[:], pgsum.rearrange("(p t) u -> p t u", t=PACK)[:, :, c * (U // 2):(c + 1) * (U // 2)])
+            pg_raw.append(raw)
+        pages = sb.tile([P, I // 16], U16, name="pages")
+        nc.sync.dma_start(pages[:], offs2)
+        val_pool = []
+        for j in range(PACK):
+            plane = sb.tile([P, T], F32, name="val_pool%d" % j)
+            nc.sync.dma_start(plane[:], vals.rearrange("(p j) t -> p j t", j=PACK)[:, j, :])
+            val_pool.append(plane)
+
+        identity = sb.tile([P, P], F32, name="identity")
+        make_identity(nc, identity[:])
+        threshold = sb.tile([P, HALVES], F32, name="threshold")
+        with nc.allow_non_contiguous_dma(reason="one threshold a partition"):
+            nc.scalar.dma_start(threshold[:], th[:, 0].rearrange("(h p) -> p h", p=P))
+        size_cols = sb.tile([P, PACK], F32, name="size_cols")
+        nc.scalar.dma_start(size_cols[:], size[0].rearrange("(p t) -> p t", t=PACK))
+        shift = sb.tile([P, HALVES], F32, name="shift")
+        nc.scalar.activation(shift[:], threshold[:], ACT.Copy, bias=-FLOOR, scale=-1.0)
+        ex = []
+        for h in range(HALVES):
+            window = sb.tile([P, U + SPARE], F32, name="ex%d" % h)
+            nc.gpsimd.memset(window[:, U:], 0.0)
+            ex.append(window)
+
+        key_words = sb.tile([P, I], U16, name="key_words", align_bytes=64)
+        nc.vector.tensor_copy(key_words[:], key_word_pool[:].indirect(slots[:]))
+        key_scales = sb.tile([P, I], U8, name="key_scales", align_bytes=64)
+        nc.vector.tensor_copy(key_scales[:], key_scale_pool[:].indirect(slots[:]))
+
+        query_grouped = sb.tile([P, Q, PACK], BF16, name="query_grouped", align_bytes=64)
+        interleave("scalar", query_grouped[:], query_raw[:])
+        query_codes, query_scales = quantise("query", query_grouped[:].rearrange("p c t -> p (c t)"), Q)
+        pquery_grouped = sb.tile([P, Q, PACK], BF16, name="pquery_grouped", align_bytes=64)
+        interleave("scalar", pquery_grouped[:], pquery_raw[:])
+
+        score = []
+        neg_max = []
+        for h in range(HALVES):
+            cols = slice(h * P, (h + 1) * P)
+            bank = ps.tile([P, I], F32, name="score%d" % h, tag="bank_a%d" % h)
+            nc.tensor.matmul_mx(out=bank[:], lhsT=query_codes[:, cols].bitcast(FP8X4), lhsT_scale=query_scales[:, cols],
+                                rhs=key_words[:].bitcast(FP4X4), rhs_scale=key_scales[:], start=True, stop=True)
+            top = sb.tile([P, 1], F32, name="neg_max%d" % h)
+            nc.vector.tensor_reduce(top[:], bank[:], mybir.AxisListType.X, ALU.max, negate=True)
+            score.append(bank)
+            neg_max.append(top)
+
+        pquery_codes, pquery_scales = quantise("pquery", pquery_grouped[:].rearrange("p c t -> p (c t)"), Q)
+        pg_grouped = sb.tile([P, U, PACK], BF16, name="pg_grouped", align_bytes=64)
+        interleave("scalar", pg_grouped[:, :U // 2, :], pg_raw[0][:])
+        interleave("vector", pg_grouped[:, U // 2:, :], pg_raw[1][:])
+
+        expo = []
+        for h in range(HALVES):
+            tile = sb.tile([P, I], F32, name="expo%d" % h)
+            nc.scalar.activation(tile[:], score[h][:], ACT.Exp, bias=neg_max[h][:], scale=1.0)
+            expo.append(tile)
+
+        pg_codes, pg_scales = quantise("pg", pg_grouped[:].rearrange("p c t -> p (c t)"), U)
+        for h in range(HALVES):
+            cols = slice(h * P, (h + 1) * P)
+            bank = ps.tile([P, U], F32, name="page_score%d" % h, tag="bank_b%d" % h)
+            nc.tensor.matmul_mx(out=bank[:], lhsT=pquery_codes[:, cols].bitcast(FP8X4), lhsT_scale=pquery_scales[:, cols],
+                                rhs=pg_codes[:].bitcast(FP8X4), rhs_scale=pg_scales[:], start=True, stop=True)
+            above = sb.tile([P, U], F32, name="above%d" % h)
+            nc.scalar.activation(above[:], bank[:], ACT.Relu, bias=shift[:, h:h + 1], scale=1.0)
+            nc.scalar.activation(ex[h][:, :U], above[:], ACT.Copy, bias=FLOOR, scale=1.0)
+
+        size_rows = ps.tile([P, PACK, P], F32, name="size_rows", tag="bank_size")
+        for t in range(PACK):
+            nc.tensor.transpose(size_rows[:, t, :], size_cols[:, t:t + 1].to_broadcast([P, P]), identity[:])
+
+        def turn_values(j):
+            picked = sb.tile([P, I], BF16, name="picked%d" % j, align_bytes=64)
+            nc.vector.tensor_copy(picked[:], val_pool[j][:].indirect(slots[:]))
+            words = picked[:].bitcast(F32)
+            turned = ps.tile([P, 2, P], F32, name="turned%d" % j, tag="bank_v%d" % (j % 3))
+            for u in range(2):
+                nc.tensor.transpose(turned[:, u, :], words[:, u::2], identity[:])
+            grouped = sb.tile([P, P * PACK], BF16, name="val_grouped%d" % j, align_bytes=64)
+            nc.scalar.copy(grouped[:].bitcast(F32).rearrange("p (c u) -> p c u", u=2),
+                           turned[:].rearrange("p u c -> p c u"))
+            return grouped
+
+        val_grouped = [turn_values(0)]
+
+        w_turned = ps.tile([P, HALVES, 2, P], F32, name="w_turned", tag="bank_b0")
+        for h in range(HALVES):
+            prob = sb.tile([P, I], F32, name="prob%d" % h)
+            nc.vector.tensor_tensor(prob[:], ex[h][:].indirect(pages[:]), expo[h][:], ALU.mult)
+            total = sb.tile([P, 1], F32, name="total%d" % h)
+            nc.scalar.activation(expo[h][:], prob[:], ACT.Copy, accum_out=total[:])
+            val_grouped.append(turn_values(h + 1))
+            inverse = sb.tile([P, 1], F32, name="inverse%d" % h)
+            nc.vector.reciprocal(inverse[:], total[:])
+            weight = sb.tile([P, I], BF16, name="weight%d" % h, align_bytes=64)
+            nc.vector.scalar_tensor_tensor(weight[:].rearrange("p (n t) -> p n t", t=PACK),
+                                           prob[:].rearrange("p (n t) -> p n t", t=PACK), inverse[:],
+                                           size_rows[:].rearrange("p t n -> p n t"), ALU.mult, ALU.mult)
+            words = weight[:].bitcast(F32)
+            for u in range(2):
+                nc.tensor.transpose(w_turned[:, h, u, :], words[:, u::2], identity[:])
+        w_grouped = sb.tile([P, Q * PACK], BF16, name="w_grouped", align_bytes=64)
+        nc.scalar.copy(w_grouped[:].bitcast(F32).rearrange("p (h c u) -> p h c u", h=HALVES, u=2),
+                       w_turned[:].rearrange("p h u c -> p h c u"))
+        w_codes, w_scales = quantise("w", w_grouped[:], Q)
+
+        result = [ps.tile([P, PACK, P], F32, name="result%d" % h, tag="bank_a%d" % h) for h in range(HALVES)]
+        out_rows = out_0.rearrange("(p j) q -> p j q", j=PACK)
+
+        def multiply(j):
+            codes, scales = quantise("val%d" % j, val_grouped[j][:], P)
+            for h in range(HALVES):
+                cols = slice(h * P, (h + 1) * P)
+                nc.tensor.matmul_mx(out=result[h][:, j, :], lhsT=codes[:].bitcast(FP8X4), lhsT_scale=scales[:],
+                                    rhs=w_codes[:, cols].bitcast(FP8X4), rhs_scale=w_scales[:, cols],
+                                    start=True, stop=True)
+
+        for j in range(PACK - 1):
+            multiply(j)
+        early = sb.tile([P, PACK - 1, Q], F32, name="early")
+        for h in range(HALVES):
+            nc.scalar.copy(early[:, :, h * P:(h + 1) * P], result[h][:, :PACK - 1, :])
+        nc.sync.dma_start(out_rows[:, :PACK - 1, :], early[:])
+
+        val_grouped.append(turn_values(PACK - 1))
+        multiply(PACK - 1)
+        out_grouped = sb.tile([P, Q, PACK], BF16, name="out_grouped", align_bytes=64)
+        nc.vector.tensor_copy(out_grouped[:, :P, :], result[0][:].rearrange("p j c -> p c j"))
+        nc.scalar.copy(out_grouped[:, P:, :], result[1][:].rearrange("p j c -> p c j"))
+        out_codes, out_scales = quantise("out", out_grouped[:].rearrange("p c t -> p (c t)"), Q)
+        late = sb.tile([P, Q], F32, name="late")
+        for h in range(HALVES):
+            nc.scalar.copy(late[:, h * P:(h + 1) * P], result[h][:, PACK - 1, :])
+        nc.scalar.dma_start(out_rows[:, PACK - 1, :], late[:])
+        nc.sync.dma_start(out_1[0].rearrange("p c t -> p (c t)").bitcast(I32), out_codes[:].bitcast(I32))
+        for g in range(4):
+            queue = nc.sync if g < 2 else nc.scalar
+            queue.dma_start(out_2[0, 4 * g:4 * g + 4, :].bitcast(I32), out_scales[32 * g:32 * g + 4, :].bitcast(I32))

@@ -22,6 +22,8 @@ PACK = 4
 HALVES = Q // P
 FLOOR = 0.05
 SPARE = 16
+OUT_SPLIT = 160
+PAGE_SPLIT = 320
 
 
 def tile_attend_pagethreshold_pl_kernel(tc, query, keys_words, keys_scales, pquery, pgsum, th, size, vals,
@@ -39,16 +41,25 @@ def tile_attend_pagethreshold_pl_kernel(tc, query, keys_words, keys_scales, pque
             else:
                 nc.vector.tensor_copy(dst, src)
 
-        def quantise(name, grouped, width):
-            codes = sb.tile([P, width], U32, name=name + "_codes", align_bytes=64)
+        def planes(name, width, tag=None):
+            codes = sb.tile([P, width], U32, name=name + "_codes", tag=tag or name + "_codes", align_bytes=64)
             scales = sb.tile([P, width], U8, name=name + "_scales", align_bytes=64)
-            nc.vector.quantize_mx(out=codes[:].bitcast(FP8X4), scales=scales[:], in_=grouped)
             return codes, scales
+
+        def quantise(codes, scales, grouped):
+            nc.vector.quantize_mx(out=codes.bitcast(FP8X4), scales=scales, in_=grouped)
+
+        half = [slice(h * P, (h + 1) * P) for h in range(HALVES)]
 
         key_scale_pool = sb.tile([P, T], U8, name="key_scale_pool")
         nc.vector.memset(key_scale_pool[:].bitcast(I32), 0)
         slots = sb.tile([P, I // 16], U16, name="slots")
         nc.sync.dma_start(slots[:], offs)
+        pages = sb.tile([P, I // 16], U16, name="pages")
+        nc.sync.dma_start(pages[:], offs2)
+        threshold = sb.tile([P, HALVES], F32, name="threshold")
+        with nc.allow_non_contiguous_dma(reason="one threshold a partition"):
+            nc.scalar.dma_start(threshold[:], th[:, 0].rearrange("(h p) -> p h", p=P))
         key_word_pool = sb.tile([P, T], U16, name="key_word_pool")
         nc.sync.dma_start(key_word_pool[:].bitcast(I32), keys_words[0].bitcast(I32))
         for g in range(4):
@@ -56,34 +67,26 @@ def tile_attend_pagethreshold_pl_kernel(tc, query, keys_words, keys_scales, pque
                               keys_scales[0, 4 * g:4 * g + 4, :].bitcast(I32))
         query_raw = sb.tile([P, PACK, Q], F32, name="query_raw")
         nc.sync.dma_start(query_raw[:], query.rearrange("(p t) q -> p t q", t=PACK))
-        pquery_raw = sb.tile([P, PACK, Q], F32, name="pquery_raw")
+        pg_raw = sb.tile([P, PACK, U], F32, name="pg_raw", tag="pg_raw", align_bytes=64)
+        nc.sync.dma_start(pg_raw[:], pgsum.rearrange("(p t) u -> p t u", t=PACK))
+        pquery_raw = sb.tile([P, PACK, Q], F32, name="pquery_raw", tag="pquery_raw", align_bytes=64)
         nc.sync.dma_start(pquery_raw[:], pquery.rearrange("(p t) q -> p t q", t=PACK))
-        pg_raw = []
-        for c in range(2):
-            raw = sb.tile([P, PACK, U // 2], F32, name="pg_raw%d" % c)
-            nc.sync.dma_start(raw[:], pgsum.rearrange("(p t) u -> p t u", t=PACK)[:, :, c * (U // 2):(c + 1) * (U // 2)])
-            pg_raw.append(raw)
-        pages = sb.tile([P, I // 16], U16, name="pages")
-        nc.sync.dma_start(pages[:], offs2)
         val_pool = []
         for j in range(PACK):
-            plane = sb.tile([P, T], F32, name="val_pool%d" % j)
+            plane = sb.tile([P, T], F32, name="val_pool%d" % j, tag="val_pool%d" % j, align_bytes=64)
             nc.sync.dma_start(plane[:], vals.rearrange("(p j) t -> p j t", j=PACK)[:, j, :])
             val_pool.append(plane)
+            if j == 0:
+                size_cols = sb.tile([P, PACK], F32, name="size_cols")
+                nc.sync.dma_start(size_cols[:], size[0].rearrange("(p t) -> p t", t=PACK))
 
         identity = sb.tile([P, P], F32, name="identity")
-        make_identity(nc, identity[:])
-        threshold = sb.tile([P, HALVES], F32, name="threshold")
-        with nc.allow_non_contiguous_dma(reason="one threshold a partition"):
-            nc.scalar.dma_start(threshold[:], th[:, 0].rearrange("(h p) -> p h", p=P))
-        size_cols = sb.tile([P, PACK], F32, name="size_cols")
-        nc.scalar.dma_start(size_cols[:], size[0].rearrange("(p t) -> p t", t=PACK))
-        shift = sb.tile([P, HALVES], F32, name="shift")
-        nc.scalar.activation(shift[:], threshold[:], ACT.Copy, bias=-FLOOR, scale=-1.0)
+        nc.vector.memset(identity[:], 0.0)
+        make_identity(nc, identity[:], nomemset=True)
         ex = []
         for h in range(HALVES):
-            window = sb.tile([P, U + SPARE], F32, name="ex%d" % h)
-            nc.gpsimd.memset(window[:, U:], 0.0)
+            window = sb.tile([P, U + SPARE], F32, name="ex%d" % h, tag="ex%d" % h, align_bytes=64)
+            nc.vector.memset(window[:, U:], 0.0)
             ex.append(window)
 
         key_words = sb.tile([P, I], U16, name="key_words", align_bytes=64)
@@ -91,113 +94,136 @@ def tile_attend_pagethreshold_pl_kernel(tc, query, keys_words, keys_scales, pque
         key_scales = sb.tile([P, I], U8, name="key_scales", align_bytes=64)
         nc.vector.tensor_copy(key_scales[:], key_scale_pool[:].indirect(slots[:]))
 
-        query_grouped = sb.tile([P, Q, PACK], BF16, name="query_grouped", align_bytes=64)
+        query_grouped = sb.tile([P, Q, PACK], BF16, name="query_grouped", tag="pg_grouped", align_bytes=64)
         interleave("scalar", query_grouped[:], query_raw[:])
-        query_codes, query_scales = quantise("query", query_grouped[:].rearrange("p c t -> p (c t)"), Q)
-        pquery_grouped = sb.tile([P, Q, PACK], BF16, name="pquery_grouped", align_bytes=64)
-        interleave("scalar", pquery_grouped[:], pquery_raw[:])
+        query_codes, query_scales = planes("query", Q)
+        quantise(query_codes[:], query_scales[:], query_grouped[:].rearrange("p c t -> p (c t)"))
+
+        pg_codes, pg_scales = planes("pg", U)
+        pg_grouped = sb.tile([P, U, PACK], BF16, name="pg_grouped", tag="pg_grouped", align_bytes=64)
+        interleave("vector", pg_grouped[:, :PAGE_SPLIT, :], pg_raw[:, :, :PAGE_SPLIT])
+        interleave("scalar", pg_grouped[:, PAGE_SPLIT:, :], pg_raw[:, :, PAGE_SPLIT:])
+        pquery_grouped = []
+        for h in range(HALVES):
+            grouped = sb.tile([P, P, PACK], BF16, name="pquery_grouped%d" % h, tag="pquery_grouped%d" % h, align_bytes=64)
+            interleave("scalar", grouped[:], pquery_raw[:, :, half[h]])
+            pquery_grouped.append(grouped)
+        quantise(pg_codes[:], pg_scales[:], pg_grouped[:].rearrange("p c t -> p (c t)"))
 
         score = []
-        neg_max = []
         for h in range(HALVES):
-            cols = slice(h * P, (h + 1) * P)
             bank = ps.tile([P, I], F32, name="score%d" % h, tag="bank_a%d" % h)
-            nc.tensor.matmul_mx(out=bank[:], lhsT=query_codes[:, cols].bitcast(FP8X4), lhsT_scale=query_scales[:, cols],
+            nc.tensor.matmul_mx(out=bank[:], lhsT=query_codes[:, half[h]].bitcast(FP8X4),
+                                lhsT_scale=query_scales[:, half[h]],
                                 rhs=key_words[:].bitcast(FP4X4), rhs_scale=key_scales[:], start=True, stop=True)
-            top = sb.tile([P, 1], F32, name="neg_max%d" % h)
-            nc.vector.tensor_reduce(top[:], bank[:], mybir.AxisListType.X, ALU.max, negate=True)
             score.append(bank)
-            neg_max.append(top)
 
-        pquery_codes, pquery_scales = quantise("pquery", pquery_grouped[:].rearrange("p c t -> p (c t)"), Q)
-        pg_grouped = sb.tile([P, U, PACK], BF16, name="pg_grouped", align_bytes=64)
-        interleave("scalar", pg_grouped[:, :U // 2, :], pg_raw[0][:])
-        interleave("vector", pg_grouped[:, U // 2:, :], pg_raw[1][:])
-
-        expo = []
+        page_score = []
         for h in range(HALVES):
-            tile = sb.tile([P, I], F32, name="expo%d" % h)
-            nc.scalar.activation(tile[:], score[h][:], ACT.Exp, bias=neg_max[h][:], scale=1.0)
-            expo.append(tile)
-
-        pg_codes, pg_scales = quantise("pg", pg_grouped[:].rearrange("p c t -> p (c t)"), U)
-        for h in range(HALVES):
-            cols = slice(h * P, (h + 1) * P)
+            codes, scales = planes("pquery%d" % h, P)
+            quantise(codes[:], scales[:], pquery_grouped[h][:].rearrange("p c t -> p (c t)"))
             bank = ps.tile([P, U], F32, name="page_score%d" % h, tag="bank_b%d" % h)
-            nc.tensor.matmul_mx(out=bank[:], lhsT=pquery_codes[:, cols].bitcast(FP8X4), lhsT_scale=pquery_scales[:, cols],
+            nc.tensor.matmul_mx(out=bank[:], lhsT=codes[:].bitcast(FP8X4), lhsT_scale=scales[:],
                                 rhs=pg_codes[:].bitcast(FP8X4), rhs_scale=pg_scales[:], start=True, stop=True)
-            above = sb.tile([P, U], F32, name="above%d" % h)
-            nc.scalar.activation(above[:], bank[:], ACT.Relu, bias=shift[:, h:h + 1], scale=1.0)
-            nc.scalar.activation(ex[h][:, :U], above[:], ACT.Copy, bias=FLOOR, scale=1.0)
+            page_score.append(bank)
 
         size_rows = ps.tile([P, PACK, P], F32, name="size_rows", tag="bank_size")
         for t in range(PACK):
             nc.tensor.transpose(size_rows[:, t, :], size_cols[:, t:t + 1].to_broadcast([P, P]), identity[:])
 
-        def turn_values(j):
-            picked = sb.tile([P, I], BF16, name="picked%d" % j, align_bytes=64)
-            nc.vector.tensor_copy(picked[:], val_pool[j][:].indirect(slots[:]))
+        expo = []
+        for h in range(HALVES):
+            top = sb.tile([P, 1], F32, name="neg_max%d" % h, tag=("pg_raw", "pg_grouped")[h], align_bytes=64)
+            nc.vector.tensor_reduce(top[:], score[h][:], mybir.AxisListType.X, ALU.max, negate=True)
+            tile = sb.tile([P, I], F32, name="expo%d" % h, tag=("pquery_raw", "expo1")[h], align_bytes=64)
+            nc.scalar.activation(tile[:], score[h][:], ACT.Exp, bias=top[:], scale=1.0)
+            expo.append(tile)
+
+        for h in range(HALVES):
+            nc.vector.tensor_scalar(ex[h][:, :U], page_score[h][:], threshold[:, h:h + 1], FLOOR, ALU.subtract, ALU.max)
+
+        def turn_values(j, picked, grouped):
             words = picked[:].bitcast(F32)
             turned = ps.tile([P, 2, P], F32, name="turned%d" % j, tag="bank_v%d" % (j % 3))
             for u in range(2):
                 nc.tensor.transpose(turned[:, u, :], words[:, u::2], identity[:])
-            grouped = sb.tile([P, P * PACK], BF16, name="val_grouped%d" % j, align_bytes=64)
-            nc.scalar.copy(grouped[:].bitcast(F32).rearrange("p (c u) -> p c u", u=2),
+            nc.scalar.copy(grouped.bitcast(F32).rearrange("p (c u) -> p c u", u=2),
                            turned[:].rearrange("p u c -> p c u"))
-            return grouped
 
-        val_grouped = [turn_values(0)]
+        def pick_values(j):
+            picked = sb.tile([P, I], BF16, name="picked%d" % j, tag="ex0" if j == 1 else "picked%d" % j, align_bytes=64)
+            nc.vector.tensor_copy(picked[:], val_pool[j][:].indirect(slots[:]))
+            return picked
 
-        w_turned = ps.tile([P, HALVES, 2, P], F32, name="w_turned", tag="bank_b0")
+        rounded_pool = sb.tile([P, T], BF16, name="rounded_pool", tag="pg_grouped", align_bytes=64)
+        nc.scalar.activation(rounded_pool[:], val_pool[0][:], ACT.Copy)
+
+        prob = []
+        total = sb.tile([P, HALVES], F32, name="total")
         for h in range(HALVES):
-            prob = sb.tile([P, I], F32, name="prob%d" % h)
-            nc.vector.tensor_tensor(prob[:], ex[h][:].indirect(pages[:]), expo[h][:], ALU.mult)
-            total = sb.tile([P, 1], F32, name="total%d" % h)
-            nc.scalar.activation(expo[h][:], prob[:], ACT.Copy, accum_out=total[:])
-            val_grouped.append(turn_values(h + 1))
-            inverse = sb.tile([P, 1], F32, name="inverse%d" % h)
-            nc.vector.reciprocal(inverse[:], total[:])
+            tile = sb.tile([P, I], F32, name="prob%d" % h)
+            nc.vector.tensor_tensor(tile[:], ex[h][:].indirect(pages[:]), expo[h][:], ALU.mult)
+            nc.scalar.activation(expo[h][:], tile[:], ACT.Copy, accum_out=total[:, h:h + 1])
+            prob.append(tile)
+
+        picked_first = sb.tile([P, I], BF16, name="picked0", tag="expo1", align_bytes=64)
+        nc.scalar.activation(picked_first[:], rounded_pool[:].indirect(slots[:]), ACT.Copy)
+
+        joint = sb.tile([P, (Q + 2 * P) * PACK], BF16, name="joint", tag="joint", align_bytes=64)
+        turn_values(1, pick_values(1), joint[:, (Q + P) * PACK:])
+        turn_values(0, picked_first, joint[:, Q * PACK:(Q + P) * PACK])
+        w_turned = ps.tile([P, HALVES, 2, P], F32, name="w_turned", tag="bank_b0")
+        inverse = sb.tile([P, HALVES], F32, name="inverse", tag="val_pool1", align_bytes=64)
+        nc.vector.reciprocal(inverse[:], total[:])
+        for h in range(HALVES):
             weight = sb.tile([P, I], BF16, name="weight%d" % h, align_bytes=64)
             nc.vector.scalar_tensor_tensor(weight[:].rearrange("p (n t) -> p n t", t=PACK),
-                                           prob[:].rearrange("p (n t) -> p n t", t=PACK), inverse[:],
+                                           prob[h][:].rearrange("p (n t) -> p n t", t=PACK), inverse[:, h:h + 1],
                                            size_rows[:].rearrange("p t n -> p n t"), ALU.mult, ALU.mult)
             words = weight[:].bitcast(F32)
             for u in range(2):
                 nc.tensor.transpose(w_turned[:, h, u, :], words[:, u::2], identity[:])
-        w_grouped = sb.tile([P, Q * PACK], BF16, name="w_grouped", align_bytes=64)
-        nc.scalar.copy(w_grouped[:].bitcast(F32).rearrange("p (h c u) -> p h c u", h=HALVES, u=2),
+        nc.scalar.copy(joint[:, :Q * PACK].bitcast(F32).rearrange("p (h c u) -> p h c u", h=HALVES, u=2),
                        w_turned[:].rearrange("p h u c -> p h c u"))
-        w_codes, w_scales = quantise("w", w_grouped[:], Q)
 
-        result = [ps.tile([P, PACK, P], F32, name="result%d" % h, tag="bank_a%d" % h) for h in range(HALVES)]
+        late_grouped = []
+        for j in (2, 3):
+            grouped = sb.tile([P, P * PACK], BF16, name="val_grouped%d" % j, align_bytes=64)
+            turn_values(j, pick_values(j), grouped[:])
+            late_grouped.append(grouped)
+
+        joint_codes, joint_scales = planes("joint", Q + 2 * P, tag="val_pool3")
+        quantise(joint_codes[:], joint_scales[:], joint[:])
+
         out_rows = out_0.rearrange("(p j) q -> p j q", j=PACK)
+        full = sb.tile([P, PACK, Q], F32, name="full")
 
-        def multiply(j):
-            codes, scales = quantise("val%d" % j, val_grouped[j][:], P)
-            for h in range(HALVES):
-                cols = slice(h * P, (h + 1) * P)
-                nc.tensor.matmul_mx(out=result[h][:, j, :], lhsT=codes[:].bitcast(FP8X4), lhsT_scale=scales[:],
-                                    rhs=w_codes[:, cols].bitcast(FP8X4), rhs_scale=w_scales[:, cols],
-                                    start=True, stop=True)
+        def multiply(j, codes, scales):
+            bank = ps.tile([P, Q], F32, name="result%d" % j, tag=("bank_a0", "bank_a1", "bank_b1", "bank_size")[j])
+            nc.tensor.matmul_mx(out=bank[:], lhsT=codes.bitcast(FP8X4), lhsT_scale=scales,
+                                rhs=joint_codes[:, :Q].bitcast(FP8X4), rhs_scale=joint_scales[:, :Q],
+                                start=True, stop=True)
+            if j == PACK - 1:
+                nc.vector.tensor_copy(full[:, j, :], bank[:])
+            else:
+                nc.scalar.copy(full[:, j, :], bank[:])
 
-        for j in range(PACK - 1):
-            multiply(j)
-        early = sb.tile([P, PACK - 1, Q], F32, name="early")
-        for h in range(HALVES):
-            nc.scalar.copy(early[:, :, h * P:(h + 1) * P], result[h][:, :PACK - 1, :])
-        nc.sync.dma_start(out_rows[:, :PACK - 1, :], early[:])
+        for j in (0, 1):
+            cols = slice(Q + j * P, Q + (j + 1) * P)
+            multiply(j, joint_codes[:, cols], joint_scales[:, cols])
+        nc.sync.dma_start(out_rows[:, :2, :], full[:, :2, :])
+        for j in (2, 3):
+            codes, scales = planes("val%d" % j, P, tag="joint" if j == 2 else None)
+            quantise(codes[:], scales[:], late_grouped[j - 2][:])
+            multiply(j, codes[:], scales[:])
+        nc.sync.dma_start(out_rows[:, 2:, :], full[:, 2:, :])
 
-        val_grouped.append(turn_values(PACK - 1))
-        multiply(PACK - 1)
         out_grouped = sb.tile([P, Q, PACK], BF16, name="out_grouped", align_bytes=64)
-        nc.vector.tensor_copy(out_grouped[:, :P, :], result[0][:].rearrange("p j c -> p c j"))
-        nc.scalar.copy(out_grouped[:, P:, :], result[1][:].rearrange("p j c -> p c j"))
-        out_codes, out_scales = quantise("out", out_grouped[:].rearrange("p c t -> p (c t)"), Q)
-        late = sb.tile([P, Q], F32, name="late")
-        for h in range(HALVES):
-            nc.scalar.copy(late[:, h * P:(h + 1) * P], result[h][:, PACK - 1, :])
-        nc.scalar.dma_start(out_rows[:, PACK - 1, :], late[:])
+        interleave("vector", out_grouped[:, :OUT_SPLIT, :], full[:, :, :OUT_SPLIT])
+        interleave("scalar", out_grouped[:, OUT_SPLIT:, :], full[:, :, OUT_SPLIT:])
+        out_codes, out_scales = planes("out", Q)
+        quantise(out_codes[:], out_scales[:], out_grouped[:].rearrange("p c t -> p (c t)"))
         nc.sync.dma_start(out_1[0].rearrange("p c t -> p (c t)").bitcast(I32), out_codes[:].bitcast(I32))
         for g in range(4):
-            queue = nc.sync if g < 2 else nc.scalar
+            queue = nc.sync if g < 1 else nc.scalar
             queue.dma_start(out_2[0, 4 * g:4 * g + 4, :].bitcast(I32), out_scales[32 * g:32 * g + 4, :].bitcast(I32))

from contextlib import ExitStack

import concourse.mybir as mybir
from concourse.masks import make_identity

D, T, I, Q, E, U = 512, 2048, 512, 256, 512, 512
FLOPS = 2 * D * Q * U + 2 * D * Q * I + 2 * I * E * Q

F32 = mybir.dt.float32
BF16 = mybir.dt.bfloat16
I32 = mybir.dt.int32
U32 = mybir.dt.uint32
U16 = mybir.dt.uint16
U8 = mybir.dt.uint8
FP8X4 = mybir.dt.float8_e4m3fn_x4
FP4X4 = mybir.dt.float4_e2m1fn_x4
ALU = mybir.AluOpType
ACT = mybir.ActivationFunctionType

P = 128
PACK = 4
HALVES = Q // P
FLOOR = 0.05
SPARE = 16
OUT_SPLIT = 160
PAGE_SPLIT = 320


def tile_attend_pagethreshold_pl_kernel(tc, query, keys_words, keys_scales, pquery, pgsum, th, size, vals,
                                         offs, offs2, out_0, out_1, out_2):
    nc = tc.nc
    with ExitStack() as ctx:
        sb = ctx.enter_context(tc.tile_pool(name="sb", bufs=1))
        ps = ctx.enter_context(tc.psum_pool(name="ps", bufs=1))

        def interleave(engine, grouped, raw):
            dst = grouped.rearrange("p (c i) t -> p c t i", i=4)
            src = raw.rearrange("p t (c i) -> p c t i", i=4)
            if engine == "scalar":
                nc.scalar.activation(dst, src, ACT.Copy)
            else:
                nc.vector.tensor_copy(dst, src)

        def planes(name, width, tag=None):
            codes = sb.tile([P, width], U32, name=name + "_codes", tag=tag or name + "_codes", align_bytes=64)
            scales = sb.tile([P, width], U8, name=name + "_scales", align_bytes=64)
            return codes, scales

        def quantise(codes, scales, grouped):
            nc.vector.quantize_mx(out=codes.bitcast(FP8X4), scales=scales, in_=grouped)

        half = [slice(h * P, (h + 1) * P) for h in range(HALVES)]

        key_scale_pool = sb.tile([P, T], U8, name="key_scale_pool")
        nc.vector.memset(key_scale_pool[:].bitcast(I32), 0)
        slots = sb.tile([P, I // 16], U16, name="slots")
        nc.sync.dma_start(slots[:], offs)
        pages = sb.tile([P, I // 16], U16, name="pages")
        nc.sync.dma_start(pages[:], offs2)
        threshold = sb.tile([P, HALVES], F32, name="threshold")
        with nc.allow_non_contiguous_dma(reason="one threshold a partition"):
            nc.scalar.dma_start(threshold[:], th[:, 0].rearrange("(h p) -> p h", p=P))
        key_word_pool = sb.tile([P, T], U16, name="key_word_pool")
        nc.sync.dma_start(key_word_pool[:].bitcast(I32), keys_words[0].bitcast(I32))
        for g in range(4):
            nc.sync.dma_start(key_scale_pool[32 * g:32 * g + 4, :].bitcast(I32),
                              keys_scales[0, 4 * g:4 * g + 4, :].bitcast(I32))
        query_raw = sb.tile([P, PACK, Q], F32, name="query_raw")
        nc.sync.dma_start(query_raw[:], query.rearrange("(p t) q -> p t q", t=PACK))
        pg_raw = sb.tile([P, PACK, U], F32, name="pg_raw", tag="pg_raw", align_bytes=64)
        nc.sync.dma_start(pg_raw[:], pgsum.rearrange("(p t) u -> p t u", t=PACK))
        pquery_raw = sb.tile([P, PACK, Q], F32, name="pquery_raw", tag="pquery_raw", align_bytes=64)
        nc.sync.dma_start(pquery_raw[:], pquery.rearrange("(p t) q -> p t q", t=PACK))
        val_pool = []
        for j in range(PACK):
            plane = sb.tile([P, T], F32, name="val_pool%d" % j, tag="val_pool%d" % j, align_bytes=64)
            nc.sync.dma_start(plane[:], vals.rearrange("(p j) t -> p j t", j=PACK)[:, j, :])
            val_pool.append(plane)
            if j == 0:
                size_cols = sb.tile([P, PACK], F32, name="size_cols")
                nc.sync.dma_start(size_cols[:], size[0].rearrange("(p t) -> p t", t=PACK))

        identity = sb.tile([P, P], F32, name="identity")
        nc.vector.memset(identity[:], 0.0)
        make_identity(nc, identity[:], nomemset=True)
        ex = []
        for h in range(HALVES):
            window = sb.tile([P, U + SPARE], F32, name="ex%d" % h, tag="ex%d" % h, align_bytes=64)
            nc.vector.memset(window[:, U:], 0.0)
            ex.append(window)

        key_words = sb.tile([P, I], U16, name="key_words", align_bytes=64)
        nc.vector.tensor_copy(key_words[:], key_word_pool[:].indirect(slots[:]))
        key_scales = sb.tile([P, I], U8, name="key_scales", align_bytes=64)
        nc.vector.tensor_copy(key_scales[:], key_scale_pool[:].indirect(slots[:]))

        query_grouped = sb.tile([P, Q, PACK], BF16, name="query_grouped", tag="pg_grouped", align_bytes=64)
        interleave("scalar", query_grouped[:], query_raw[:])
        query_codes, query_scales = planes("query", Q)
        quantise(query_codes[:], query_scales[:], query_grouped[:].rearrange("p c t -> p (c t)"))

        pg_codes, pg_scales = planes("pg", U)
        pg_grouped = sb.tile([P, U, PACK], BF16, name="pg_grouped", tag="pg_grouped", align_bytes=64)
        interleave("vector", pg_grouped[:, :PAGE_SPLIT, :], pg_raw[:, :, :PAGE_SPLIT])
        interleave("scalar", pg_grouped[:, PAGE_SPLIT:, :], pg_raw[:, :, PAGE_SPLIT:])
        pquery_grouped = []
        for h in range(HALVES):
            grouped = sb.tile([P, P, PACK], BF16, name="pquery_grouped%d" % h, tag="pquery_grouped%d" % h, align_bytes=64)
            interleave("scalar", grouped[:], pquery_raw[:, :, half[h]])
            pquery_grouped.append(grouped)
        quantise(pg_codes[:], pg_scales[:], pg_grouped[:].rearrange("p c t -> p (c t)"))

        score = []
        for h in range(HALVES):
            bank = ps.tile([P, I], F32, name="score%d" % h, tag="bank_a%d" % h)
            nc.tensor.matmul_mx(out=bank[:], lhsT=query_codes[:, half[h]].bitcast(FP8X4),
                                lhsT_scale=query_scales[:, half[h]],
                                rhs=key_words[:].bitcast(FP4X4), rhs_scale=key_scales[:], start=True, stop=True)
            score.append(bank)

        page_score = []
        for h in range(HALVES):
            codes, scales = planes("pquery%d" % h, P)
            quantise(codes[:], scales[:], pquery_grouped[h][:].rearrange("p c t -> p (c t)"))
            bank = ps.tile([P, U], F32, name="page_score%d" % h, tag="bank_b%d" % h)
            nc.tensor.matmul_mx(out=bank[:], lhsT=codes[:].bitcast(FP8X4), lhsT_scale=scales[:],
                                rhs=pg_codes[:].bitcast(FP8X4), rhs_scale=pg_scales[:], start=True, stop=True)
            page_score.append(bank)

        size_rows = ps.tile([P, PACK, P], F32, name="size_rows", tag="bank_size")
        for t in range(PACK):
            nc.tensor.transpose(size_rows[:, t, :], size_cols[:, t:t + 1].to_broadcast([P, P]), identity[:])

        expo = []
        for h in range(HALVES):
            top = sb.tile([P, 1], F32, name="neg_max%d" % h, tag=("pg_raw", "pg_grouped")[h], align_bytes=64)
            nc.vector.tensor_reduce(top[:], score[h][:], mybir.AxisListType.X, ALU.max, negate=True)
            tile = sb.tile([P, I], F32, name="expo%d" % h, tag=("pquery_raw", "expo1")[h], align_bytes=64)
            nc.scalar.activation(tile[:], score[h][:], ACT.Exp, bias=top[:], scale=1.0)
            expo.append(tile)

        for h in range(HALVES):
            nc.vector.tensor_scalar(ex[h][:, :U], page_score[h][:], threshold[:, h:h + 1], FLOOR, ALU.subtract, ALU.max)

        def turn_values(j, picked, grouped):
            words = picked[:].bitcast(F32)
            turned = ps.tile([P, 2, P], F32, name="turned%d" % j, tag="bank_v%d" % (j % 3))
            for u in range(2):
                nc.tensor.transpose(turned[:, u, :], words[:, u::2], identity[:])
            nc.scalar.copy(grouped.bitcast(F32).rearrange("p (c u) -> p c u", u=2),
                           turned[:].rearrange("p u c -> p c u"))

        def pick_values(j):
            picked = sb.tile([P, I], BF16, name="picked%d" % j, tag="ex0" if j == 1 else "picked%d" % j, align_bytes=64)
            nc.vector.tensor_copy(picked[:], val_pool[j][:].indirect(slots[:]))
            return picked

        rounded_pool = sb.tile([P, T], BF16, name="rounded_pool", tag="pg_grouped", align_bytes=64)
        nc.scalar.activation(rounded_pool[:], val_pool[0][:], ACT.Copy)

        prob = []
        total = sb.tile([P, HALVES], F32, name="total")
        for h in range(HALVES):
            tile = sb.tile([P, I], F32, name="prob%d" % h)
            nc.vector.tensor_tensor(tile[:], ex[h][:].indirect(pages[:]), expo[h][:], ALU.mult)
            nc.scalar.activation(expo[h][:], tile[:], ACT.Copy, accum_out=total[:, h:h + 1])
            prob.append(tile)

        picked_first = sb.tile([P, I], BF16, name="picked0", tag="expo1", align_bytes=64)
        nc.scalar.activation(picked_first[:], rounded_pool[:].indirect(slots[:]), ACT.Copy)

        joint = sb.tile([P, (Q + 2 * P) * PACK], BF16, name="joint", tag="joint", align_bytes=64)
        turn_values(1, pick_values(1), joint[:, (Q + P) * PACK:])
        turn_values(0, picked_first, joint[:, Q * PACK:(Q + P) * PACK])
        w_turned = ps.tile([P, HALVES, 2, P], F32, name="w_turned", tag="bank_b0")
        inverse = sb.tile([P, HALVES], F32, name="inverse", tag="val_pool1", align_bytes=64)
        nc.vector.reciprocal(inverse[:], total[:])
        for h in range(HALVES):
            weight = sb.tile([P, I], BF16, name="weight%d" % h, align_bytes=64)
            nc.vector.scalar_tensor_tensor(weight[:].rearrange("p (n t) -> p n t", t=PACK),
                                           prob[h][:].rearrange("p (n t) -> p n t", t=PACK), inverse[:, h:h + 1],
                                           size_rows[:].rearrange("p t n -> p n t"), ALU.mult, ALU.mult)
            words = weight[:].bitcast(F32)
            for u in range(2):
                nc.tensor.transpose(w_turned[:, h, u, :], words[:, u::2], identity[:])
        nc.scalar.copy(joint[:, :Q * PACK].bitcast(F32).rearrange("p (h c u) -> p h c u", h=HALVES, u=2),
                       w_turned[:].rearrange("p h u c -> p h c u"))

        late_grouped = []
        for j in (2, 3):
            grouped = sb.tile([P, P * PACK], BF16, name="val_grouped%d" % j, align_bytes=64)
            turn_values(j, pick_values(j), grouped[:])
            late_grouped.append(grouped)

        joint_codes, joint_scales = planes("joint", Q + 2 * P, tag="val_pool3")
        quantise(joint_codes[:], joint_scales[:], joint[:])

        out_rows = out_0.rearrange("(p j) q -> p j q", j=PACK)
        full = sb.tile([P, PACK, Q], F32, name="full")

        def multiply(j, codes, scales):
            bank = ps.tile([P, Q], F32, name="result%d" % j, tag=("bank_a0", "bank_a1", "bank_b1", "bank_size")[j])
            nc.tensor.matmul_mx(out=bank[:], lhsT=codes.bitcast(FP8X4), lhsT_scale=scales,
                                rhs=joint_codes[:, :Q].bitcast(FP8X4), rhs_scale=joint_scales[:, :Q],
                                start=True, stop=True)
            if j == PACK - 1:
                nc.vector.tensor_copy(full[:, j, :], bank[:])
            else:
                nc.scalar.copy(full[:, j, :], bank[:])

        for j in (0, 1):
            cols = slice(Q + j * P, Q + (j + 1) * P)
            multiply(j, joint_codes[:, cols], joint_scales[:, cols])
        nc.sync.dma_start(out_rows[:, :2, :], full[:, :2, :])
        for j in (2, 3):
            codes, scales = planes("val%d" % j, P, tag="joint" if j == 2 else None)
            quantise(codes[:], scales[:], late_grouped[j - 2][:])
            multiply(j, codes[:], scales[:])
        nc.sync.dma_start(out_rows[:, 2:, :], full[:, 2:, :])

        out_grouped = sb.tile([P, Q, PACK], BF16, name="out_grouped", align_bytes=64)
        interleave("vector", out_grouped[:, :OUT_SPLIT, :], full[:, :, :OUT_SPLIT])
        interleave("scalar", out_grouped[:, OUT_SPLIT:, :], full[:, :, OUT_SPLIT:])
        out_codes, out_scales = planes("out", Q)
        quantise(out_codes[:], out_scales[:], out_grouped[:].rearrange("p c t -> p (c t)"))
        nc.sync.dma_start(out_1[0].rearrange("p c t -> p (c t)").bitcast(I32), out_codes[:].bitcast(I32))
        for g in range(4):
            queue = nc.sync if g < 1 else nc.scalar
            queue.dma_start(out_2[0, 4 * g:4 * g + 4, :].bitcast(I32), out_scales[32 * g:32 * g + 4, :].bitcast(I32))
